import numpy as np
import ml_dtypes


def mxq(x, axis, fmt="e4m3"):
    dtype, down = {"e4m3": (ml_dtypes.float8_e4m3fn, 7), "e5m2": (ml_dtypes.float8_e5m2, 14)}[fmt]
    v = np.moveaxis(np.asarray(x, np.float32).astype(ml_dtypes.bfloat16).astype(np.float64), axis, -1)
    blocks = v.reshape(v.shape[:-1] + (-1, 32))
    amax = np.abs(blocks).max(-1, keepdims=True)
    byte = np.maximum(np.where(amax > 0, np.frexp(amax)[1] - 1 + 127, 0) - down, 1)
    scale = np.exp2(byte - 127.0)
    codes = (blocks / scale).astype(np.float32).astype(dtype).astype(np.float64)
    return np.moveaxis((codes * scale).reshape(v.shape), -1, axis)


WIDE = False


def mx_kscale(k):
    if not WIDE:
        return np.ones(k)
    levels = np.array([10, -10, 5, -5, 0])
    if k % 512:
        return np.exp2(np.random.permutation(np.resize(levels, k // 32))).repeat(32)
    a = np.empty((k // 512, 16))
    for p in range(k // 512):
        a[p, :8] = np.random.permutation(np.resize(levels, 8))
        for g in range(8):
            far = levels[np.abs(levels - a[p, g]) >= 10]
            a[p, g + 8] = far[np.random.randint(len(far))]
    return np.exp2(a.ravel()).repeat(32)


def f64(x):
    return np.asarray(x).astype(np.float64)


def striped(idx):
    return np.tile(idx.reshape(-1, 16).T, (8, 1)).astype(np.uint16)


def unstriped(offs):
    return offs[:16].T.reshape(-1).astype(np.int64)


def pack_weight(w):
    k, n = w.shape
    w = f64(np.asarray(w, np.float32).astype(ml_dtypes.bfloat16)).reshape(k // 32, 32, n)
    amax = np.abs(w).max(1)
    byte = np.clip(np.where(amax > 0, np.frexp(amax)[1] - 1 + 127 - 7, 1), 1, 254)
    scaled = (w * np.exp2(127.0 - byte)[:, None, :]).reshape(k, n).astype(np.float32)
    words = np.ascontiguousarray(scaled.reshape(k // 512, 128, 4, n).transpose(0, 1, 3, 2)).astype(ml_dtypes.float8_e4m3fn).view(np.uint8)
    return words, np.ascontiguousarray(byte.astype(np.uint8).reshape(k // 512, 16, n))


def unpack_weight(words, scales):
    g, p, n, _ = words.shape
    vals = np.ascontiguousarray(words).view(ml_dtypes.float8_e4m3fn).astype(np.float64) * np.repeat(np.exp2(scales.astype(np.float64) - 127.0), 8, axis=1)[..., None]
    return vals.transpose(0, 1, 3, 2).reshape(g * 512, n)


K, T, S, N, R = 1024, 1024, 512, 256, 256
P = 2 ** 7


def setup_inputs():
    n = np.random.standard_normal
    s = mx_kscale(K)[:, None]
    packed_xT = pack_weight(n((K, T)) * s)
    return {
        "x_words": packed_xT[0],
        "x_scales": packed_xT[1],
        "w1": (n((K, N)) / np.sqrt(K) / s).astype(np.float32),
        "w2": (n((K, N)) / np.sqrt(K) / s).astype(np.float32),
        "mcon": (np.random.uniform(0.2, 3.0, (N, R))).astype(np.float32),
        "lfc": (np.tile(-np.random.uniform(0.3, 1.2, S), (P, 1))).astype(np.float32),
        "offs": striped(np.random.permutation(T)[:S]),
        "bath": striped(np.random.permutation(np.concatenate([np.arange(R), np.random.randint(0, R, S - R)]))),
    }


def reference(x_words, x_scales, w1, w2, mcon, lfc, offs, bath):
    xq = unpack_weight(x_words, x_scales)[:, unstriped(offs)]
    yi = mxq(f64(w2), 0, "e4m3").T @ xq
    yo = mxq(f64(w1), 0, "e4m3").T @ xq
    mb = f64(mcon)[:, unstriped(bath)]
    lpr = 0.8 * (yo - yi) + np.log(mb)
    lf = f64(lfc)[:1] / (((lpr - 0.4) / (-1.0 * (0.5 * f64(lfc)[:1]) + 1.0)) ** 2 + 1.0)
    return 0.8 * yi + lpr - (np.log(np.exp(lpr) + 1.0)) + lf

@@ -1,0 +1,227 @@
+import math
+from contextlib import ExitStack
+
+import concourse.mybir as mybir
+from concourse.masks import make_identity
+
+K, T, S, N, R = 1024, 1024, 512, 256, 256
+FLOPS = 2 * 2 * K * S * N
+
+F32 = mybir.dt.float32
+BF16 = mybir.dt.bfloat16
+I32 = mybir.dt.int32
+U32 = mybir.dt.uint32
+U16 = mybir.dt.uint16
+U8 = mybir.dt.uint8
+FP8X4 = mybir.dt.float8_e4m3fn_x4
+ALU = mybir.AluOpType
+ACT = mybir.ActivationFunctionType
+
+P = 128
+PACK = 4
+K_PASS = P * PACK
+PASSES = K // K_PASS
+JB = S // P
+MB = N // P
+SHIFT = 0.4
+CLAMP = 40.0
+
+
+def tile_picked_ytroef_log_p_kernel(
+    tc, x_words, x_scales, w1, w2, mcon, lfc, offs, bath, out
+):
+    nc = tc.nc
+    with ExitStack() as ctx:
+        sb = ctx.enter_context(tc.tile_pool(name="sb", bufs=1))
+        ps = ctx.enter_context(tc.psum_pool(name="ps", bufs=1))
+
+        offs_t = sb.tile([P, S // 16], U16, name="offs_t")
+        bath_t = sb.tile([P, S // 16], U16, name="bath_t")
+        m_tab = [sb.tile([P, R], F32, name="m_tab%d" % m) for m in range(MB)]
+        s_tab = sb.tile([P, T], U8, name="s_tab")
+        x_tab = [sb.tile([P, T], I32, name="x_tab%d" % g) for g in range(PASSES)]
+        w_raw = {(a, g): sb.tile([P, PACK, N], F32, name="w_raw%d%d" % (a, g), tag="w_raw%d%d" % (a, g)) for a in range(2) for g in range(PASSES)}
+        lf_col = sb.tile([P, JB], F32, name="lf_col")
+
+        warm_out = sb.tile([P, 8], F32, name="warm_out")
+        nc.gpsimd.memset(s_tab[:].bitcast(I32), 0)
+        ident = sb.tile([P, P], F32, name="ident")
+        make_identity(nc, ident[:])
+
+        def load_w(a, g):
+            w = (w1, w2)[a]
+            nc.sync.dma_start(
+                out=w_raw[a, g][:], in_=w[g * K_PASS : (g + 1) * K_PASS, :].rearrange("(p t) n -> p t n", t=PACK)
+            )
+
+        def load_x(g):
+            nc.sync.dma_start(out=x_tab[g][:], in_=x_words[g].rearrange("p n t -> p (n t)").bitcast(I32))
+
+        nc.sync.dma_start(out=m_tab[0][:], in_=mcon[0:P, :])
+        nc.sync.dma_start(bath_t[:], bath)
+        nc.sync.dma_start(out=m_tab[1][:], in_=mcon[P : 2 * P, :])
+        nc.sync.dma_start(offs_t[:], offs)
+        for q in range(4):
+            nc.sync.dma_start(
+                out=s_tab[32 * q : 32 * q + 4 * PASSES, :].bitcast(I32),
+                in_=x_scales[:, 4 * q : 4 * q + 4, :].bitcast(I32),
+            )
+        load_w(0, 0)
+        load_x(0)
+        load_w(1, 0)
+        load_w(0, 1)
+        load_w(1, 1)
+        load_x(1)
+        with nc.allow_non_contiguous_dma(reason="one factor to a partition"):
+            nc.gpsimd.dma_start(out=lf_col[:], in_=lfc[0:1, :].rearrange("o (b p) -> p (o b)", p=P))
+
+        m_log = [sb.tile([P, 3 * R], F32, name="m_log%d" % m) for m in range(MB)]
+        for m in range(MB):
+            nc.vector.memset(m_log[m][:, R:], 0.0)
+            nc.scalar.activation(m_log[m][:, :R], m_tab[m][:], ACT.Ln, scale=math.exp(-SHIFT))
+        nc.scalar.activation(warm_out[:], m_log[MB - 1][:, 0:8], ACT.Abs_reciprocal_sqrt, bias=1.0, scale=0.0)
+
+        c_col = sb.tile([P, JB], F32, name="c_col")
+        csq = sb.tile([P, JB], F32, name="csq")
+        lf_neg = sb.tile([P, JB], F32, name="lf_neg")
+        a_neg = sb.tile([P, JB], F32, name="a_neg")
+        nc.gpsimd.tensor_scalar(c_col[:], lf_col[:], -0.5, 1.0, ALU.mult, ALU.add)
+        nc.gpsimd.tensor_scalar(lf_neg[:], lf_col[:], -1.0, 0.0, ALU.mult, ALU.add)
+        nc.gpsimd.tensor_tensor(csq[:], c_col[:], c_col[:], ALU.mult)
+        nc.gpsimd.tensor_tensor(a_neg[:], csq[:], lf_neg[:], ALU.mult)
+
+        mb = [sb.tile([P, S], F32, name="mb%d" % m, tag="mb%d" % m, align_bytes=64) for m in range(MB)]
+        for m in range(MB):
+            nc.vector.tensor_copy(mb[m][:], m_log[m][:].indirect(bath_t[:]))
+        x_sc = sb.tile([P, S], U8, name="x_sc", align_bytes=64)
+        nc.vector.tensor_copy(x_sc[:], s_tab[:].indirect(offs_t[:]))
+        g_bank = []
+        for jb in range(JB):
+            g_ps = ps.tile([P, N], F32, name="g_ps%d" % jb, tag="a%d" % jb)
+            for m in range(MB):
+                nc.tensor.transpose(g_ps[:, m * P : (m + 1) * P], mb[m][:, jb * P : (jb + 1) * P], ident[:])
+            g_bank.append(g_ps)
+
+        x_cd = [sb.tile([P, S], U32, name="x_cd0", tag="mb0", align_bytes=64)]
+
+        w_bf = {k: sb.tile([P, N, PACK], BF16, name="w_bf%d%d" % k, tag="w_bf%d%d" % k, align_bytes=64) for k in w_raw}
+        w_cd = [sb.tile([P, 2 * N], U32, name="w_cd%d" % g, align_bytes=64) for g in range(PASSES)]
+        w_sc = [sb.tile([P, 2 * N], U8, name="w_sc%d" % g, align_bytes=64) for g in range(PASSES)]
+
+        def cast(copy, key, lo, hi):
+            copy(
+                w_bf[key][:, lo:hi, :].rearrange("p (c i) t -> p c t i", i=4),
+                w_raw[key][:, :, lo:hi].rearrange("p t (c i) -> p c t i", i=4),
+            )
+
+        def quant(key):
+            a, g = key
+            nc.vector.quantize_mx(
+                out=w_cd[g][:, a * N : (a + 1) * N].bitcast(FP8X4),
+                scales=w_sc[g][:, a * N : (a + 1) * N],
+                in_=w_bf[key][:].rearrange("p n t -> p (n t)"),
+            )
+
+        def gather_x(g, lo, hi):
+            nc.vector.tensor_copy(
+                x_cd[g][:, lo:hi], x_tab[g][:].bitcast(U32).indirect(offs_t[:, lo // 16 : hi // 16])
+            )
+
+        y = [ps.tile([P, 2, N], F32, name="y%d" % jb, tag="b%d" % jb) for jb in range(JB)]
+
+        def mm(g, jb):
+            cols = slice(jb * P, (jb + 1) * P)
+            nc.tensor.matmul_mx(
+                out=y[jb][:].rearrange("p a n -> p (a n)"),
+                lhsT=x_cd[g][:, cols].bitcast(FP8X4),
+                lhsT_scale=x_sc[4 * g :, cols],
+                rhs=w_cd[g][:].bitcast(FP8X4),
+                rhs_scale=w_sc[g][:],
+                start=(g == 0),
+                stop=(g == PASSES - 1),
+            )
+
+        cast(nc.scalar.copy, (0, 0), 0, N)
+        gather_x(0, 0, S)
+        quant((0, 0))
+        cast(nc.scalar.copy, (1, 0), 0, N)
+        quant((1, 0))
+        for jb in range(JB):
+            mm(0, jb)
+        cast(nc.vector.tensor_copy, (0, 1), 0, N)
+        cast(nc.scalar.copy, (1, 1), 0, N)
+        quant((0, 1))
+        quant((1, 1))
+        g_t = sb.tile([P, JB, N], F32, name="g_t", tag="w_raw11")
+        x_cd.append(sb.tile([P, S], U32, name="x_cd1", tag="w_bf11", align_bytes=64))
+        for jb in range(JB):
+            nc.scalar.copy(g_t[:, jb, :], g_bank[jb][:])
+        for jb in range(JB):
+            gather_x(1, jb * P, (jb + 1) * P)
+            mm(1, jb)
+
+        nz = sb.tile([P, JB, N], F32, name="nz")
+        lp = sb.tile([P, JB, N], F32, name="lp")
+        sq = sb.tile([P, JB, N], F32, name="sq", tag="sq")
+        rs = sb.tile([P, JB, N], F32, name="rs")
+        for jb in range(JB):
+            nc.vector.scalar_tensor_tensor(nz[:, jb, :], y[jb][:, 0, :], -0.8, g_t[:, jb, :], ALU.mult, ALU.subtract)
+            nc.vector.scalar_tensor_tensor(lp[:, jb, :], y[jb][:, 1, :], -0.8, nz[:, jb, :], ALU.mult, ALU.subtract)
+            nc.scalar.activation(sq[:, jb, :], lp[:, jb, :], ACT.Square)
+            nc.scalar.activation(rs[:, jb, :], sq[:, jb, :], ACT.Abs_reciprocal_sqrt, bias=csq[:, jb : jb + 1])
+
+        acc = {(m, h): ps.tile([P, 2, P], F32, name="acc%d%d" % (m, h), tag="a%d" % (2 * m + h)) for m in range(MB) for h in range(2)}
+
+        def add_terms(src, m, h, first, last):
+            for i in range(2):
+                nc.tensor.matmul(
+                    acc[m, h][:, i, :],
+                    src[:, 2 * h + i, m * P : (m + 1) * P],
+                    ident[:],
+                    is_transpose=True,
+                    start=first and i == 0,
+                    stop=last and i == 1,
+                )
+
+        for m in range(MB):
+            for h in range(2):
+                add_terms(nz, m, h, True, False)
+
+        ex = sb.tile([P, JB, N], F32, name="ex", tag="sq")
+        arg = sb.tile([P, JB, N], F32, name="arg")
+        nc.vector.tensor_scalar(arg[:], lp[:], SHIFT, -CLAMP, ALU.add, ALU.max)
+        for m in range(MB):
+            for h in range(2):
+                add_terms(arg, m, h, False, False)
+        nc.scalar.activation(
+            ex[:].rearrange("p b n -> p (b n)"),
+            arg[:].rearrange("p b n -> p (b n)"),
+            ACT.Exp,
+            scale=-1.0,
+        )
+        nlf = sb.tile([P, JB, N], F32, name="nlf")
+        for jb in range(JB):
+            nc.vector.scalar_tensor_tensor(
+                nlf[:, jb, :], rs[:, jb, :], a_neg[:, jb : jb + 1], rs[:, jb, :], ALU.mult, ALU.mult
+            )
+        for m in range(MB):
+            for h in range(2):
+                add_terms(nlf, m, h, False, False)
+        for m in range(MB):
+            for h in range(2):
+                soft = sb.tile([P, 2, P], F32, name="soft%d%d" % (m, h))
+                nc.scalar.activation(
+                    soft[:],
+                    ex[:, 2 * h : 2 * h + 2, m * P : (m + 1) * P],
+                    ACT.Ln,
+                    bias=1.0,
+                )
+                for i in range(2):
+                    nc.tensor.matmul(
+                        acc[m, h][:, i, :], soft[:, i, :], ident[:], is_transpose=True, start=False, stop=i == 1
+                    )
+                res = sb.tile([P, 2 * P], F32, name="res%d%d" % (m, h))
+                nc.vector.tensor_scalar(
+                    res[:], acc[m, h][:].rearrange("p i j -> p (i j)"), -1.0, SHIFT, ALU.mult, ALU.add
+                )
+                nc.sync.dma_start(out=out[m * P : (m + 1) * P, 2 * h * P : 2 * (h + 1) * P], in_=res[:])

@@ -25,6 +25,7 @@ JB = S // P
 MB = N // P
 SHIFT = 0.4
 CLAMP = 40.0
+V_SHARE = 160
 
 
 def tile_picked_ytroef_log_p_kernel(
@@ -37,14 +38,14 @@ def tile_picked_ytroef_log_p_kernel(
 
         offs_t = sb.tile([P, S // 16], U16, name="offs_t")
         bath_t = sb.tile([P, S // 16], U16, name="bath_t")
-        m_tab = [sb.tile([P, R], F32, name="m_tab%d" % m) for m in range(MB)]
+        m_tab = [sb.tile([P, R], F32, name="m_tab%d" % m, tag="m_tab%d" % m) for m in range(MB)]
         s_tab = sb.tile([P, T], U8, name="s_tab")
-        x_tab = [sb.tile([P, T], I32, name="x_tab%d" % g) for g in range(PASSES)]
-        w_raw = {(a, g): sb.tile([P, PACK, N], F32, name="w_raw%d%d" % (a, g), tag="w_raw%d%d" % (a, g)) for a in range(2) for g in range(PASSES)}
+        x_tab = [sb.tile([P, T], I32, name="x_tab0")]
+        w_raw = {(0, g): sb.tile([P, PACK, N], F32, name="w_raw0%d" % g, tag="w_raw0%d" % g) for g in range(PASSES)}
         lf_col = sb.tile([P, JB], F32, name="lf_col")
 
-        warm_out = sb.tile([P, 8], F32, name="warm_out")
-        nc.gpsimd.memset(s_tab[:].bitcast(I32), 0)
+        warm_out = sb.tile([P, 8], F32, name="warm_out", tag="warm")
+        nc.vector.memset(s_tab[:].bitcast(I32), 0)
         ident = sb.tile([P, P], F32, name="ident")
         make_identity(nc, ident[:])
 
@@ -60,18 +61,15 @@ def tile_picked_ytroef_log_p_kernel(
         nc.sync.dma_start(out=m_tab[0][:], in_=mcon[0:P, :])
         nc.sync.dma_start(bath_t[:], bath)
         nc.sync.dma_start(out=m_tab[1][:], in_=mcon[P : 2 * P, :])
+        load_w(0, 0)
         nc.sync.dma_start(offs_t[:], offs)
+        load_x(0)
+        load_w(0, 1)
         for q in range(4):
             nc.sync.dma_start(
                 out=s_tab[32 * q : 32 * q + 4 * PASSES, :].bitcast(I32),
                 in_=x_scales[:, 4 * q : 4 * q + 4, :].bitcast(I32),
             )
-        load_w(0, 0)
-        load_x(0)
-        load_w(1, 0)
-        load_w(0, 1)
-        load_w(1, 1)
-        load_x(1)
         with nc.allow_non_contiguous_dma(reason="one factor to a partition"):
             nc.gpsimd.dma_start(out=lf_col[:], in_=lfc[0:1, :].rearrange("o (b p) -> p (o b)", p=P))
 
@@ -81,6 +79,12 @@ def tile_picked_ytroef_log_p_kernel(
             nc.scalar.activation(m_log[m][:, :R], m_tab[m][:], ACT.Ln, scale=math.exp(-SHIFT))
         nc.scalar.activation(warm_out[:], m_log[MB - 1][:, 0:8], ACT.Abs_reciprocal_sqrt, bias=1.0, scale=0.0)
 
+        x_tab.append(sb.tile([P, T], I32, name="x_tab1", tag="m_tab0"))
+        w_raw[1, 0] = sb.tile([P, PACK, N], F32, name="w_raw10", tag="m_tab1")
+        w_raw[1, 1] = sb.tile([P, PACK, N], F32, name="w_raw11", tag="warm")
+        load_x(1)
+        load_w(1, 0)
+        load_w(1, 1)
         c_col = sb.tile([P, JB], F32, name="c_col")
         csq = sb.tile([P, JB], F32, name="csq")
         lf_neg = sb.tile([P, JB], F32, name="lf_neg")
@@ -93,135 +97,127 @@ def tile_picked_ytroef_log_p_kernel(
         mb = [sb.tile([P, S], F32, name="mb%d" % m, tag="mb%d" % m, align_bytes=64) for m in range(MB)]
         for m in range(MB):
             nc.vector.tensor_copy(mb[m][:], m_log[m][:].indirect(bath_t[:]))
-        x_sc = sb.tile([P, S], U8, name="x_sc", align_bytes=64)
-        nc.vector.tensor_copy(x_sc[:], s_tab[:].indirect(offs_t[:]))
-        g_bank = []
-        for jb in range(JB):
-            g_ps = ps.tile([P, N], F32, name="g_ps%d" % jb, tag="a%d" % jb)
-            for m in range(MB):
-                nc.tensor.transpose(g_ps[:, m * P : (m + 1) * P], mb[m][:, jb * P : (jb + 1) * P], ident[:])
-            g_bank.append(g_ps)
+        g_bank = [ps.tile([P, 2, N], F32, name="g_ps%d" % h, tag="b%d" % h) for h in range(2)]
+        for m in range(MB):
+            for jb in range(JB):
+                nc.tensor.transpose(
+                    g_bank[jb // 2][:, jb % 2, m * P : (m + 1) * P], mb[m][:, jb * P : (jb + 1) * P], ident[:]
+                )
 
         x_cd = [sb.tile([P, S], U32, name="x_cd0", tag="mb0", align_bytes=64)]
+        x_sc = sb.tile([P, S], U8, name="x_sc", tag="mb1", align_bytes=64)
+        w_bf = {}
+        w_cd = {k: sb.tile([P, N], U32, name="w_cd%d%d" % k, align_bytes=64) for k in w_raw}
+        w_sc = {k: sb.tile([P, N], U8, name="w_sc%d%d" % k, align_bytes=64) for k in w_raw}
 
-        w_bf = {k: sb.tile([P, N, PACK], BF16, name="w_bf%d%d" % k, tag="w_bf%d%d" % k, align_bytes=64) for k in w_raw}
-        w_cd = [sb.tile([P, 2 * N], U32, name="w_cd%d" % g, align_bytes=64) for g in range(PASSES)]
-        w_sc = [sb.tile([P, 2 * N], U8, name="w_sc%d" % g, align_bytes=64) for g in range(PASSES)]
-
-        def cast(copy, key, lo, hi):
+        def cast(copy, key, lo, hi, tag):
+            if key not in w_bf:
+                w_bf[key] = sb.tile([P, N, PACK], BF16, name="w_bf%d%d" % key, tag=tag, align_bytes=64)
             copy(
                 w_bf[key][:, lo:hi, :].rearrange("p (c i) t -> p c t i", i=4),
                 w_raw[key][:, :, lo:hi].rearrange("p t (c i) -> p c t i", i=4),
             )
 
         def quant(key):
-            a, g = key
             nc.vector.quantize_mx(
-                out=w_cd[g][:, a * N : (a + 1) * N].bitcast(FP8X4),
-                scales=w_sc[g][:, a * N : (a + 1) * N],
-                in_=w_bf[key][:].rearrange("p n t -> p (n t)"),
+                out=w_cd[key][:].bitcast(FP8X4), scales=w_sc[key][:], in_=w_bf[key][:].rearrange("p n t -> p (n t)")
             )
 
-        def gather_x(g, lo, hi):
-            nc.vector.tensor_copy(
-                x_cd[g][:, lo:hi], x_tab[g][:].bitcast(U32).indirect(offs_t[:, lo // 16 : hi // 16])
-            )
+        def gather_x(g):
+            nc.vector.tensor_copy(x_cd[g][:], x_tab[g][:].bitcast(U32).indirect(offs_t[:]))
 
-        y = [ps.tile([P, 2, N], F32, name="y%d" % jb, tag="b%d" % jb) for jb in range(JB)]
-
-        def mm(g, jb):
+        def mm(dst, a, g, jb):
             cols = slice(jb * P, (jb + 1) * P)
             nc.tensor.matmul_mx(
-                out=y[jb][:].rearrange("p a n -> p (a n)"),
+                out=dst,
                 lhsT=x_cd[g][:, cols].bitcast(FP8X4),
                 lhsT_scale=x_sc[4 * g :, cols],
-                rhs=w_cd[g][:].bitcast(FP8X4),
-                rhs_scale=w_sc[g][:],
+                rhs=w_cd[a, g][:].bitcast(FP8X4),
+                rhs_scale=w_sc[a, g][:],
                 start=(g == 0),
                 stop=(g == PASSES - 1),
             )
 
-        cast(nc.scalar.copy, (0, 0), 0, N)
-        gather_x(0, 0, S)
+        cast(nc.scalar.copy, (0, 0), 0, N, "bf_a")
+        gather_x(0)
         quant((0, 0))
-        cast(nc.scalar.copy, (1, 0), 0, N)
-        quant((1, 0))
-        for jb in range(JB):
-            mm(0, jb)
-        cast(nc.vector.tensor_copy, (0, 1), 0, N)
-        cast(nc.scalar.copy, (1, 1), 0, N)
+        nc.vector.tensor_copy(x_sc[:], s_tab[:].indirect(offs_t[:]))
+        cast(nc.scalar.copy, (0, 1), 0, N, "bf_b")
+        g_t = sb.tile([P, JB, N], F32, name="g_t", tag="w_raw01")
+        for h in range(2):
+            nc.scalar.copy(g_t[:, 2 * h : 2 * h + 2, :], g_bank[h][:])
+        x_cd.append(sb.tile([P, S], U32, name="x_cd1", tag="bf_a", align_bytes=64))
+        gather_x(1)
         quant((0, 1))
+        yo = [ps.tile([P, N], F32, name="yo%d" % jb, tag="a%d" % jb) for jb in range(JB)]
+        yi = [ps.tile([P, N], F32, name="yi%d" % jb, tag="b%d" % jb) for jb in range(JB)]
+        for g in range(PASSES):
+            for jb in range(JB):
+                mm(yo[jb][:], 0, g, jb)
+        cast(nc.scalar.copy, (1, 0), 0, N, "bf_c")
+        quant((1, 0))
+        cast(nc.vector.tensor_copy, (1, 1), 0, V_SHARE, "bf_b")
+        cast(nc.scalar.copy, (1, 1), V_SHARE, N, "bf_b")
         quant((1, 1))
-        g_t = sb.tile([P, JB, N], F32, name="g_t", tag="w_raw11")
-        x_cd.append(sb.tile([P, S], U32, name="x_cd1", tag="w_bf11", align_bytes=64))
         for jb in range(JB):
-            nc.scalar.copy(g_t[:, jb, :], g_bank[jb][:])
-        for jb in range(JB):
-            gather_x(1, jb * P, (jb + 1) * P)
-            mm(1, jb)
+            for g in range(PASSES):
+                mm(yi[jb][:], 1, g, jb)
 
-        nz = sb.tile([P, JB, N], F32, name="nz")
+        nz = sb.tile([P, JB, N], F32, name="nz", tag="bf_b", align_bytes=64)
         lp = sb.tile([P, JB, N], F32, name="lp")
         sq = sb.tile([P, JB, N], F32, name="sq", tag="sq")
         rs = sb.tile([P, JB, N], F32, name="rs")
+
+        def make_nz(jb):
+            nc.vector.scalar_tensor_tensor(nz[:, jb, :], yo[jb][:], -0.8, g_t[:, jb, :], ALU.mult, ALU.subtract)
+
+        make_nz(0)
         for jb in range(JB):
-            nc.vector.scalar_tensor_tensor(nz[:, jb, :], y[jb][:, 0, :], -0.8, g_t[:, jb, :], ALU.mult, ALU.subtract)
-            nc.vector.scalar_tensor_tensor(lp[:, jb, :], y[jb][:, 1, :], -0.8, nz[:, jb, :], ALU.mult, ALU.subtract)
-            nc.scalar.activation(sq[:, jb, :], lp[:, jb, :], ACT.Square)
+            if jb + 1 < JB:
+                make_nz(jb + 1)
+            nc.vector.scalar_tensor_tensor(lp[:, jb, :], yi[jb][:], -0.8, nz[:, jb, :], ALU.mult, ALU.subtract)
+            if jb + 1 < JB:
+                nc.scalar.activation(sq[:, jb, :], lp[:, jb, :], ACT.Square)
+            else:
+                nc.vector.tensor_tensor(sq[:, jb, :], lp[:, jb, :], lp[:, jb, :], ALU.mult)
             nc.scalar.activation(rs[:, jb, :], sq[:, jb, :], ACT.Abs_reciprocal_sqrt, bias=csq[:, jb : jb + 1])
 
-        acc = {(m, h): ps.tile([P, 2, P], F32, name="acc%d%d" % (m, h), tag="a%d" % (2 * m + h)) for m in range(MB) for h in range(2)}
-
-        def add_terms(src, m, h, first, last):
-            for i in range(2):
-                nc.tensor.matmul(
-                    acc[m, h][:, i, :],
-                    src[:, 2 * h + i, m * P : (m + 1) * P],
-                    ident[:],
-                    is_transpose=True,
-                    start=first and i == 0,
-                    stop=last and i == 1,
-                )
-
-        for m in range(MB):
-            for h in range(2):
-                add_terms(nz, m, h, True, False)
-
-        ex = sb.tile([P, JB, N], F32, name="ex", tag="sq")
         arg = sb.tile([P, JB, N], F32, name="arg")
-        nc.vector.tensor_scalar(arg[:], lp[:], SHIFT, -CLAMP, ALU.add, ALU.max)
+        nc.vector.tensor_scalar(arg[:], lp[:], -(CLAMP + SHIFT), None, ALU.max)
+        arg_t = [ps.tile([P, JB, P], F32, name="arg_t%d" % m, tag="b%d" % m) for m in range(MB)]
         for m in range(MB):
-            for h in range(2):
-                add_terms(arg, m, h, False, False)
-        nc.scalar.activation(
-            ex[:].rearrange("p b n -> p (b n)"),
-            arg[:].rearrange("p b n -> p (b n)"),
-            ACT.Exp,
-            scale=-1.0,
-        )
+            for jb in range(JB):
+                nc.tensor.transpose(arg_t[m][:, jb, :], arg[:, jb, m * P : (m + 1) * P], ident[:])
+        ex = sb.tile([P, MB, S], F32, name="ex", tag="sq")
+        for m in range(MB):
+            nc.scalar.activation(
+                ex[:, m, :], arg_t[m][:].rearrange("p b j -> p (b j)"), ACT.Exp, scale=-1.0, bias=-SHIFT
+            )
+
         nlf = sb.tile([P, JB, N], F32, name="nlf")
         for jb in range(JB):
             nc.vector.scalar_tensor_tensor(
                 nlf[:, jb, :], rs[:, jb, :], a_neg[:, jb : jb + 1], rs[:, jb, :], ALU.mult, ALU.mult
             )
-        for m in range(MB):
-            for h in range(2):
-                add_terms(nlf, m, h, False, False)
-        for m in range(MB):
-            for h in range(2):
-                soft = sb.tile([P, 2, P], F32, name="soft%d%d" % (m, h))
-                nc.scalar.activation(
-                    soft[:],
-                    ex[:, 2 * h : 2 * h + 2, m * P : (m + 1) * P],
-                    ACT.Ln,
-                    bias=1.0,
-                )
+        pieces = [(m, h) for m in range(MB) for h in range(2)]
+        acc = {(m, h): ps.tile([P, 2, P], F32, name="acc%d%d" % (m, h), tag="a%d" % (2 * m + h)) for m, h in pieces}
+        for term, src in enumerate((nz, arg, nlf)):
+            for m, h in pieces:
                 for i in range(2):
                     nc.tensor.matmul(
-                        acc[m, h][:, i, :], soft[:, i, :], ident[:], is_transpose=True, start=False, stop=i == 1
+                        acc[m, h][:, i, :],
+                        src[:, 2 * h + i, m * P : (m + 1) * P],
+                        ident[:],
+                        is_transpose=True,
+                        start=term == 0 and i == 0,
+                        stop=term == 2 and i == 1,
                     )
-                res = sb.tile([P, 2 * P], F32, name="res%d%d" % (m, h))
-                nc.vector.tensor_scalar(
-                    res[:], acc[m, h][:].rearrange("p i j -> p (i j)"), -1.0, SHIFT, ALU.mult, ALU.add
-                )
-                nc.sync.dma_start(out=out[m * P : (m + 1) * P, 2 * h * P : 2 * (h + 1) * P], in_=res[:])
+        for m, h in pieces:
+            cols = slice(2 * h * P, 2 * (h + 1) * P)
+            soft = sb.tile([P, 2 * P], F32, name="soft%d%d" % (m, h))
+            nc.scalar.activation(soft[:], ex[:, m, cols], ACT.Ln, bias=1.0)
+            res = sb.tile([P, 2 * P], F32, name="res%d%d" % (m, h))
+            nc.vector.scalar_tensor_tensor(
+                res[:], acc[m, h][:].rearrange("p i j -> p (i j)"), -1.0, soft[:], ALU.mult, ALU.subtract
+            )
+            nc.sync.dma_start(out=out[m * P : (m + 1) * P, cols], in_=res[:])

@@ -2,7 +2,6 @@ import math
 from contextlib import ExitStack
 
 import concourse.mybir as mybir
-from concourse.masks import make_identity
 
 K, T, S, N, R = 1024, 1024, 512, 256, 256
 FLOPS = 2 * 2 * K * S * N
@@ -39,7 +38,7 @@ def tile_picked_ytroef_log_p_kernel(
         offs_t = sb.tile([P, S // 16], U16, name="offs_t")
         bath_t = sb.tile([P, S // 16], U16, name="bath_t")
         m_tab = [sb.tile([P, R], F32, name="m_tab%d" % m, tag="m_tab%d" % m) for m in range(MB)]
-        s_tab = sb.tile([P, T], U8, name="s_tab")
+        s_tab = sb.tile([P, T], U8, name="s_tab", tag="scales", align_bytes=64)
         x_tab = [sb.tile([P, T], I32, name="x_tab0")]
         w_raw = {(0, g): sb.tile([P, PACK, N], F32, name="w_raw0%d" % g, tag="w_raw0%d" % g) for g in range(PASSES)}
         lf_col = sb.tile([P, JB], F32, name="lf_col")
@@ -47,7 +46,16 @@ def tile_picked_ytroef_log_p_kernel(
         warm_out = sb.tile([P, 8], F32, name="warm_out", tag="warm")
         nc.vector.memset(s_tab[:].bitcast(I32), 0)
         ident = sb.tile([P, P], F32, name="ident")
-        make_identity(nc, ident[:])
+        ones = sb.tile([P, P], F32, name="ones")
+        col = sb.tile([P, P], F32, name="col", align_bytes=64)
+        lane = sb.tile([P, 32], F32, name="lane", align_bytes=64)
+        base = sb.tile([P, 1], F32, name="base")
+        nc.vector.memset(ones[:], 1.0)
+        for q in range(4):
+            nc.vector.memset(base[32 * q : 32 * (q + 1), :], 32.0 * q)
+        nc.vector.tensor_tensor_scan(col[:], ones[:], ones[:], -1.0, ALU.mult, ALU.add)
+        nc.vector.transpose(lane[:], col[:, 0:32])
+        nc.vector.tensor_scalar(ident[:], col[:], base[:, 0:1], lane[:, 0:1], ALU.subtract, ALU.is_equal)
 
         def load_w(a, g):
             w = (w1, w2)[a]
@@ -94,7 +102,7 @@ def tile_picked_ytroef_log_p_kernel(
         nc.gpsimd.tensor_tensor(csq[:], c_col[:], c_col[:], ALU.mult)
         nc.gpsimd.tensor_tensor(a_neg[:], csq[:], lf_neg[:], ALU.mult)
 
-        mb = [sb.tile([P, S], F32, name="mb%d" % m, tag="mb%d" % m, align_bytes=64) for m in range(MB)]
+        mb = [sb.tile([P, S], F32, name="mb%d" % m) for m in range(MB)]
         for m in range(MB):
             nc.vector.tensor_copy(mb[m][:], m_log[m][:].indirect(bath_t[:]))
         g_bank = [ps.tile([P, 2, N], F32, name="g_ps%d" % h, tag="b%d" % h) for h in range(2)]
@@ -104,11 +112,11 @@ def tile_picked_ytroef_log_p_kernel(
                     g_bank[jb // 2][:, jb % 2, m * P : (m + 1) * P], mb[m][:, jb * P : (jb + 1) * P], ident[:]
                 )
 
-        x_cd = [sb.tile([P, S], U32, name="x_cd0", tag="mb0", align_bytes=64)]
-        x_sc = sb.tile([P, S], U8, name="x_sc", tag="mb1", align_bytes=64)
+        x_cd = [sb.tile([P, S], U32, name="x_cd0", align_bytes=64)]
+        x_sc = sb.tile([P, S], U8, name="x_sc", align_bytes=64)
         w_bf = {}
+        w_sc = {}
         w_cd = {k: sb.tile([P, N], U32, name="w_cd%d%d" % k, align_bytes=64) for k in w_raw}
-        w_sc = {k: sb.tile([P, N], U8, name="w_sc%d%d" % k, align_bytes=64) for k in w_raw}
 
         def cast(copy, key, lo, hi, tag):
             if key not in w_bf:
@@ -120,7 +128,7 @@ def tile_picked_ytroef_log_p_kernel(
 
         def quant(key):
             nc.vector.quantize_mx(
-                out=w_cd[key][:].bitcast(FP8X4), scales=w_sc[key][:], in_=w_bf[key][:].rearrange("p n t -> p (n t)")
+                out=w_cd[key][:].bitcast(FP8X4), scales=w_sc[key], in_=w_bf[key][:].rearrange("p n t -> p (n t)")
             )
 
         def gather_x(g):
@@ -133,15 +141,18 @@ def tile_picked_ytroef_log_p_kernel(
                 lhsT=x_cd[g][:, cols].bitcast(FP8X4),
                 lhsT_scale=x_sc[4 * g :, cols],
                 rhs=w_cd[a, g][:].bitcast(FP8X4),
-                rhs_scale=w_sc[a, g][:],
+                rhs_scale=w_sc[a, g],
                 start=(g == 0),
                 stop=(g == PASSES - 1),
             )
 
         cast(nc.scalar.copy, (0, 0), 0, N, "bf_a")
         gather_x(0)
-        quant((0, 0))
         nc.vector.tensor_copy(x_sc[:], s_tab[:].indirect(offs_t[:]))
+        w_planes = sb.tile([P, 2 * PASSES * N], U8, name="w_planes", tag="scales", align_bytes=64)
+        for n, key in enumerate(sorted(w_raw)):
+            w_sc[key] = w_planes[:, n * N : (n + 1) * N]
+        quant((0, 0))
         cast(nc.scalar.copy, (0, 1), 0, N, "bf_b")
         g_t = sb.tile([P, JB, N], F32, name="g_t", tag="w_raw01")
         for h in range(2):
@@ -184,7 +195,7 @@ def tile_picked_ytroef_log_p_kernel(
 
         arg = sb.tile([P, JB, N], F32, name="arg")
         nc.vector.tensor_scalar(arg[:], lp[:], -(CLAMP + SHIFT), None, ALU.max)
-        arg_t = [ps.tile([P, JB, P], F32, name="arg_t%d" % m, tag="b%d" % m) for m in range(MB)]
+        arg_t = [ps.tile([P, JB, P], F32, name="arg_t%d" % m, tag="a%d" % m) for m in range(MB)]
         for m in range(MB):
             for jb in range(JB):
                 nc.tensor.transpose(arg_t[m][:, jb, :], arg[:, jb, m * P : (m + 1) * P], ident[:])
@@ -200,17 +211,17 @@ def tile_picked_ytroef_log_p_kernel(
                 nlf[:, jb, :], rs[:, jb, :], a_neg[:, jb : jb + 1], rs[:, jb, :], ALU.mult, ALU.mult
             )
         pieces = [(m, h) for m in range(MB) for h in range(2)]
-        acc = {(m, h): ps.tile([P, 2, P], F32, name="acc%d%d" % (m, h), tag="a%d" % (2 * m + h)) for m, h in pieces}
+        acc = [ps.tile([P, JB, P], F32, name="acc%d" % m, tag="b%d" % (2 + m)) for m in range(MB)]
         for term, src in enumerate((nz, arg, nlf)):
-            for m, h in pieces:
-                for i in range(2):
+            for m in range(MB):
+                for jb in range(JB):
                     nc.tensor.matmul(
-                        acc[m, h][:, i, :],
-                        src[:, 2 * h + i, m * P : (m + 1) * P],
+                        acc[m][:, jb, :],
+                        src[:, jb, m * P : (m + 1) * P],
                         ident[:],
                         is_transpose=True,
-                        start=term == 0 and i == 0,
-                        stop=term == 2 and i == 1,
+                        start=term == 0 and jb == 0,
+                        stop=term == 2 and jb == JB - 1,
                     )
         for m, h in pieces:
             cols = slice(2 * h * P, 2 * (h + 1) * P)
@@ -218,6 +229,6 @@ def tile_picked_ytroef_log_p_kernel(
             nc.scalar.activation(soft[:], ex[:, m, cols], ACT.Ln, bias=1.0)
             res = sb.tile([P, 2 * P], F32, name="res%d%d" % (m, h))
             nc.vector.scalar_tensor_tensor(
-                res[:], acc[m, h][:].rearrange("p i j -> p (i j)"), -1.0, soft[:], ALU.mult, ALU.subtract
+                res[:], acc[m][:].rearrange("p b j -> p (b j)")[:, cols], -1.0, soft[:], ALU.mult, ALU.subtract
             )
             nc.sync.dma_start(out=out[m * P : (m + 1) * P, cols], in_=res[:])

@@ -25,6 +25,7 @@ MB = N // P
 SHIFT = 0.4
 CLAMP = 40.0
 V_SHARE = 160
+WINDOW = 704
 
 
 def tile_picked_ytroef_log_p_kernel(
@@ -37,14 +38,18 @@ def tile_picked_ytroef_log_p_kernel(
 
         offs_t = sb.tile([P, S // 16], U16, name="offs_t")
         bath_t = sb.tile([P, S // 16], U16, name="bath_t")
-        m_tab = [sb.tile([P, R], F32, name="m_tab%d" % m, tag="m_tab%d" % m) for m in range(MB)]
+        m_tab = [sb.tile([P, R], F32, name="m_tab%d" % m) for m in range(MB)]
         s_tab = sb.tile([P, T], U8, name="s_tab", tag="scales", align_bytes=64)
-        x_tab = [sb.tile([P, T], I32, name="x_tab0")]
-        w_raw = {(0, g): sb.tile([P, PACK, N], F32, name="w_raw0%d" % g, tag="w_raw0%d" % g) for g in range(PASSES)}
+        x_tab = [sb.tile([P, T], I32, name="x_tab%d" % g) for g in range(PASSES)]
+        w_raw = {
+            (a, g): sb.tile([P, PACK, N], F32, name="w_raw%d%d" % (a, g), tag="w_raw%d%d" % (a, g))
+            for a in range(2)
+            for g in range(PASSES)
+        }
         lf_col = sb.tile([P, JB], F32, name="lf_col")
 
-        warm_out = sb.tile([P, 8], F32, name="warm_out", tag="warm")
-        nc.vector.memset(s_tab[:].bitcast(I32), 0)
+        warm_out = sb.tile([P, 8], F32, name="warm_out")
+        nc.gpsimd.memset(s_tab[:].bitcast(I32), 0)
         ident = sb.tile([P, P], F32, name="ident")
         ones = sb.tile([P, P], F32, name="ones")
         col = sb.tile([P, P], F32, name="col", align_bytes=64)
@@ -74,37 +79,27 @@ def tile_picked_ytroef_log_p_kernel(
         load_x(0)
         load_w(0, 1)
         for q in range(4):
-            nc.sync.dma_start(
+            nc.gpsimd.dma_start(
                 out=s_tab[32 * q : 32 * q + 4 * PASSES, :].bitcast(I32),
                 in_=x_scales[:, 4 * q : 4 * q + 4, :].bitcast(I32),
             )
-        with nc.allow_non_contiguous_dma(reason="one factor to a partition"):
-            nc.gpsimd.dma_start(out=lf_col[:], in_=lfc[0:1, :].rearrange("o (b p) -> p (o b)", p=P))
-
-        m_log = [sb.tile([P, 3 * R], F32, name="m_log%d" % m) for m in range(MB)]
-        for m in range(MB):
-            nc.vector.memset(m_log[m][:, R:], 0.0)
-            nc.scalar.activation(m_log[m][:, :R], m_tab[m][:], ACT.Ln, scale=math.exp(-SHIFT))
-        nc.scalar.activation(warm_out[:], m_log[MB - 1][:, 0:8], ACT.Abs_reciprocal_sqrt, bias=1.0, scale=0.0)
-
-        x_tab.append(sb.tile([P, T], I32, name="x_tab1", tag="m_tab0"))
-        w_raw[1, 0] = sb.tile([P, PACK, N], F32, name="w_raw10", tag="m_tab1")
-        w_raw[1, 1] = sb.tile([P, PACK, N], F32, name="w_raw11", tag="warm")
         load_x(1)
         load_w(1, 0)
         load_w(1, 1)
-        c_col = sb.tile([P, JB], F32, name="c_col")
-        csq = sb.tile([P, JB], F32, name="csq")
-        lf_neg = sb.tile([P, JB], F32, name="lf_neg")
-        a_neg = sb.tile([P, JB], F32, name="a_neg")
-        nc.gpsimd.tensor_scalar(c_col[:], lf_col[:], -0.5, 1.0, ALU.mult, ALU.add)
-        nc.gpsimd.tensor_scalar(lf_neg[:], lf_col[:], -1.0, 0.0, ALU.mult, ALU.add)
-        nc.gpsimd.tensor_tensor(csq[:], c_col[:], c_col[:], ALU.mult)
-        nc.gpsimd.tensor_tensor(a_neg[:], csq[:], lf_neg[:], ALU.mult)
+        with nc.allow_non_contiguous_dma(reason="one factor to a partition"):
+            nc.sync.dma_start(out=lf_col[:], in_=lfc[0:1, :].rearrange("o (b p) -> p (o b)", p=P))
+
+        m_log = sb.tile([P, R + WINDOW], F32, name="m_log")
+        nc.vector.memset(m_log[:, MB * R :], 0.0)
+        m_at = [(MB - 1 - m) * R for m in range(MB)]
+        for m in range(MB):
+            nc.scalar.activation(m_log[:, m_at[m] : m_at[m] + R], m_tab[m][:], ACT.Ln, scale=math.exp(-SHIFT))
+        nc.scalar.activation(warm_out[:], m_log[:, 0:8], ACT.Abs_reciprocal_sqrt, bias=1.0, scale=0.0)
+
 
         mb = [sb.tile([P, S], F32, name="mb%d" % m) for m in range(MB)]
         for m in range(MB):
-            nc.vector.tensor_copy(mb[m][:], m_log[m][:].indirect(bath_t[:]))
+            nc.vector.tensor_copy(mb[m][:], m_log[:, m_at[m] : m_at[m] + WINDOW].indirect(bath_t[:]))
         g_bank = [ps.tile([P, 2, N], F32, name="g_ps%d" % h, tag="b%d" % h) for h in range(2)]
         for m in range(MB):
             for jb in range(JB):
@@ -174,6 +169,9 @@ def tile_picked_ytroef_log_p_kernel(
             for g in range(PASSES):
                 mm(yi[jb][:], 1, g, jb)
 
+        csq = sb.tile([P, JB], F32, name="csq", tag="w_raw11")
+        a_neg = sb.tile([P, JB], F32, name="a_neg")
+        nc.scalar.activation(csq[:], lf_col[:], ACT.Square, scale=-0.5, bias=1.0)
         nz = sb.tile([P, JB, N], F32, name="nz", tag="bf_b", align_bytes=64)
         lp = sb.tile([P, JB, N], F32, name="lp")
         sq = sb.tile([P, JB, N], F32, name="sq", tag="sq")
@@ -205,6 +203,7 @@ def tile_picked_ytroef_log_p_kernel(
                 ex[:, m, :], arg_t[m][:].rearrange("p b j -> p (b j)"), ACT.Exp, scale=-1.0, bias=-SHIFT
             )
 
+        nc.vector.scalar_tensor_tensor(a_neg[:], csq[:], -1.0, lf_col[:], ALU.mult, ALU.mult)
         nlf = sb.tile([P, JB, N], F32, name="nlf")
         for jb in range(JB):
             nc.vector.scalar_tensor_tensor(

@@ -17,15 +17,18 @@ ALU = mybir.AluOpType
 ACT = mybir.ActivationFunctionType
 
 P = 128
+QUAD = 32
 PACK = 4
 K_PASS = P * PACK
 PASSES = K // K_PASS
 JB = S // P
 MB = N // P
+LINE = 4
 SHIFT = 0.4
 CLAMP = 40.0
-V_SHARE = 160
 WINDOW = 704
+V_SHARE = 160
+W1, W2 = 0, 1
 
 
 def tile_picked_ytroef_log_p_kernel(
@@ -36,98 +39,103 @@ def tile_picked_ytroef_log_p_kernel(
         sb = ctx.enter_context(tc.tile_pool(name="sb", bufs=1))
         ps = ctx.enter_context(tc.psum_pool(name="ps", bufs=1))
 
+        s_tab = sb.tile([P, T], U8, name="s_tab", tag="scales", align_bytes=64)
+        nc.vector.memset(s_tab[:].bitcast(I32), 0)
+
+        ident = sb.tile([P, P], F32, name="ident")
+        ones = sb.tile([P, P], F32, name="ones", tag="stage_a")
+        col = sb.tile([P, P], F32, name="col", tag="stage_b", align_bytes=64)
+        lane = sb.tile([P, QUAD], F32, name="lane", align_bytes=64)
+        quad_base = sb.tile([P, 1], F32, name="quad_base")
+        nc.vector.memset(ones[:], 1.0)
+        for q in range(P // QUAD):
+            nc.vector.memset(quad_base[QUAD * q : QUAD * (q + 1), :], float(QUAD * q))
+        nc.vector.tensor_tensor_scan(col[:], ones[:], ones[:], -1.0, ALU.mult, ALU.add)
+        nc.vector.transpose(lane[:], col[:, 0:QUAD])
+        nc.vector.tensor_scalar(ident[:], col[:], quad_base[:, 0:1], lane[:, 0:1], ALU.subtract, ALU.is_equal)
+
         offs_t = sb.tile([P, S // 16], U16, name="offs_t")
         bath_t = sb.tile([P, S // 16], U16, name="bath_t")
-        m_tab = [sb.tile([P, R], F32, name="m_tab%d" % m) for m in range(MB)]
-        s_tab = sb.tile([P, T], U8, name="s_tab", tag="scales", align_bytes=64)
-        x_tab = [sb.tile([P, T], I32, name="x_tab%d" % g) for g in range(PASSES)]
-        w_raw = {
-            (a, g): sb.tile([P, PACK, N], F32, name="w_raw%d%d" % (a, g), tag="w_raw%d%d" % (a, g))
-            for a in range(2)
-            for g in range(PASSES)
-        }
+        m_tab = [sb.tile([P, R], F32, name="m_tab%d" % m, tag="stage_m%d" % m) for m in range(MB)]
         lf_col = sb.tile([P, JB], F32, name="lf_col")
+        x_tab = {}
+        w_raw = {}
 
-        warm_out = sb.tile([P, 8], F32, name="warm_out")
-        nc.gpsimd.memset(s_tab[:].bitcast(I32), 0)
-        ident = sb.tile([P, P], F32, name="ident")
-        ones = sb.tile([P, P], F32, name="ones")
-        col = sb.tile([P, P], F32, name="col", align_bytes=64)
-        lane = sb.tile([P, 32], F32, name="lane", align_bytes=64)
-        base = sb.tile([P, 1], F32, name="base")
-        nc.vector.memset(ones[:], 1.0)
-        for q in range(4):
-            nc.vector.memset(base[32 * q : 32 * (q + 1), :], 32.0 * q)
-        nc.vector.tensor_tensor_scan(col[:], ones[:], ones[:], -1.0, ALU.mult, ALU.add)
-        nc.vector.transpose(lane[:], col[:, 0:32])
-        nc.vector.tensor_scalar(ident[:], col[:], base[:, 0:1], lane[:, 0:1], ALU.subtract, ALU.is_equal)
+        def load_w(a, g, tag):
+            w_raw[a, g] = sb.tile([P, PACK, N], F32, name="w_raw%d%d" % (a, g), tag=tag)
+            rows = (w1, w2)[a][g * K_PASS : (g + 1) * K_PASS, :]
+            nc.sync.dma_start(out=w_raw[a, g][:], in_=rows.rearrange("(p t) n -> p t n", t=PACK))
 
-        def load_w(a, g):
-            w = (w1, w2)[a]
-            nc.sync.dma_start(
-                out=w_raw[a, g][:], in_=w[g * K_PASS : (g + 1) * K_PASS, :].rearrange("(p t) n -> p t n", t=PACK)
-            )
-
-        def load_x(g):
+        def load_x(g, tag):
+            x_tab[g] = sb.tile([P, T], I32, name="x_tab%d" % g, tag=tag, align_bytes=64)
             nc.sync.dma_start(out=x_tab[g][:], in_=x_words[g].rearrange("p n t -> p (n t)").bitcast(I32))
 
         nc.sync.dma_start(out=m_tab[0][:], in_=mcon[0:P, :])
         nc.sync.dma_start(bath_t[:], bath)
         nc.sync.dma_start(out=m_tab[1][:], in_=mcon[P : 2 * P, :])
-        load_w(0, 0)
+        load_w(W1, 0, "w_first")
         nc.sync.dma_start(offs_t[:], offs)
-        load_x(0)
-        load_w(0, 1)
-        for q in range(4):
-            nc.gpsimd.dma_start(
-                out=s_tab[32 * q : 32 * q + 4 * PASSES, :].bitcast(I32),
+        load_x(0, "x_first")
+        for q in range(P // QUAD):
+            nc.sync.dma_start(
+                out=s_tab[QUAD * q : QUAD * q + 4 * PASSES, :].bitcast(I32),
                 in_=x_scales[:, 4 * q : 4 * q + 4, :].bitcast(I32),
             )
-        load_x(1)
-        load_w(1, 0)
-        load_w(1, 1)
+        load_w(W1, 1, "stage_a")
+        load_x(1, "stage_b")
         with nc.allow_non_contiguous_dma(reason="one factor to a partition"):
-            nc.sync.dma_start(out=lf_col[:], in_=lfc[0:1, :].rearrange("o (b p) -> p (o b)", p=P))
+            nc.gpsimd.dma_start(out=lf_col[:], in_=lfc[0:1, :].rearrange("o (b p) -> p (o b)", p=P))
 
         m_log = sb.tile([P, R + WINDOW], F32, name="m_log")
         nc.vector.memset(m_log[:, MB * R :], 0.0)
         m_at = [(MB - 1 - m) * R for m in range(MB)]
         for m in range(MB):
             nc.scalar.activation(m_log[:, m_at[m] : m_at[m] + R], m_tab[m][:], ACT.Ln, scale=math.exp(-SHIFT))
-        nc.scalar.activation(warm_out[:], m_log[:, 0:8], ACT.Abs_reciprocal_sqrt, bias=1.0, scale=0.0)
+        load_w(W2, 0, "stage_m0")
+        load_w(W2, 1, "stage_m1")
 
-
-        mb = [sb.tile([P, S], F32, name="mb%d" % m) for m in range(MB)]
+        log_mb = [sb.tile([P, S], F32, name="log_mb%d" % m) for m in range(MB)]
         for m in range(MB):
-            nc.vector.tensor_copy(mb[m][:], m_log[:, m_at[m] : m_at[m] + WINDOW].indirect(bath_t[:]))
-        g_bank = [ps.tile([P, 2, N], F32, name="g_ps%d" % h, tag="b%d" % h) for h in range(2)]
+            nc.vector.tensor_copy(log_mb[m][:], m_log[:, m_at[m] : m_at[m] + WINDOW].indirect(bath_t[:]))
+        log_bank = [ps.tile([P, 2, N], F32, name="log_bank%d" % h, tag="b%d" % h) for h in range(JB // 2)]
         for m in range(MB):
             for jb in range(JB):
                 nc.tensor.transpose(
-                    g_bank[jb // 2][:, jb % 2, m * P : (m + 1) * P], mb[m][:, jb * P : (jb + 1) * P], ident[:]
+                    log_bank[jb // 2][:, jb % 2, m * P : (m + 1) * P],
+                    log_mb[m][:, jb * P : (jb + 1) * P],
+                    ident[:],
                 )
 
-        x_cd = [sb.tile([P, S], U32, name="x_cd0", align_bytes=64)]
+        x_cd = {}
         x_sc = sb.tile([P, S], U8, name="x_sc", align_bytes=64)
         w_bf = {}
-        w_sc = {}
-        w_cd = {k: sb.tile([P, N], U32, name="w_cd%d%d" % k, align_bytes=64) for k in w_raw}
+        w_cd = {key: sb.tile([P, N], U32, name="w_cd%d%d" % key, align_bytes=64) for key in sorted(w_raw)}
 
-        def cast(copy, key, lo, hi, tag):
-            if key not in w_bf:
-                w_bf[key] = sb.tile([P, N, PACK], BF16, name="w_bf%d%d" % key, tag=tag, align_bytes=64)
+        def new_bf(key, tag):
+            w_bf[key] = sb.tile([P, N, PACK], BF16, name="w_bf%d%d" % key, tag=tag, align_bytes=64)
+
+        def cast(copy, key, lo, hi):
             copy(
-                w_bf[key][:, lo:hi, :].rearrange("p (c i) t -> p c t i", i=4),
-                w_raw[key][:, :, lo:hi].rearrange("p t (c i) -> p c t i", i=4),
+                w_bf[key][:, lo:hi, :].rearrange("p (c i) t -> p c t i", i=LINE),
+                w_raw[key][:, :, lo:hi].rearrange("p t (c i) -> p c t i", i=LINE),
             )
+
+        def gather_x(g, tag):
+            x_cd[g] = sb.tile([P, S], U32, name="x_cd%d" % g, tag=tag, align_bytes=64)
+            nc.vector.tensor_copy(x_cd[g][:], x_tab[g][:].bitcast(U32).indirect(offs_t[:]))
+
+        new_bf((W1, 0), "bf_a")
+        cast(nc.scalar.copy, (W1, 0), 0, N)
+        gather_x(0, "x_codes")
+        nc.vector.tensor_copy(x_sc[:], s_tab[:].indirect(offs_t[:]))
+
+        w_scales = sb.tile([P, 2 * PASSES * N], U8, name="w_scales", tag="scales", align_bytes=64)
+        w_sc = {key: w_scales[:, n * N : (n + 1) * N] for n, key in enumerate(sorted(w_raw))}
 
         def quant(key):
             nc.vector.quantize_mx(
                 out=w_cd[key][:].bitcast(FP8X4), scales=w_sc[key], in_=w_bf[key][:].rearrange("p n t -> p (n t)")
             )
-
-        def gather_x(g):
-            nc.vector.tensor_copy(x_cd[g][:], x_tab[g][:].bitcast(U32).indirect(offs_t[:]))
 
         def mm(dst, a, g, jb):
             cols = slice(jb * P, (jb + 1) * P)
@@ -141,93 +149,95 @@ def tile_picked_ytroef_log_p_kernel(
                 stop=(g == PASSES - 1),
             )
 
-        cast(nc.scalar.copy, (0, 0), 0, N, "bf_a")
-        gather_x(0)
-        nc.vector.tensor_copy(x_sc[:], s_tab[:].indirect(offs_t[:]))
-        w_planes = sb.tile([P, 2 * PASSES * N], U8, name="w_planes", tag="scales", align_bytes=64)
-        for n, key in enumerate(sorted(w_raw)):
-            w_sc[key] = w_planes[:, n * N : (n + 1) * N]
-        quant((0, 0))
-        cast(nc.scalar.copy, (0, 1), 0, N, "bf_b")
-        g_t = sb.tile([P, JB, N], F32, name="g_t", tag="w_raw01")
-        for h in range(2):
-            nc.scalar.copy(g_t[:, 2 * h : 2 * h + 2, :], g_bank[h][:])
-        x_cd.append(sb.tile([P, S], U32, name="x_cd1", tag="bf_a", align_bytes=64))
-        gather_x(1)
-        quant((0, 1))
+        quant((W1, 0))
+        new_bf((W1, 1), "bf_b")
+        cast(nc.scalar.copy, (W1, 1), 0, N)
+        log_t = sb.tile([P, JB, N], F32, name="log_t", tag="stage_a")
+        for h in range(JB // 2):
+            nc.scalar.copy(log_t[:, 2 * h : 2 * h + 2, :], log_bank[h][:])
+        gather_x(1, "bf_a")
+        quant((W1, 1))
         yo = [ps.tile([P, N], F32, name="yo%d" % jb, tag="a%d" % jb) for jb in range(JB)]
         yi = [ps.tile([P, N], F32, name="yi%d" % jb, tag="b%d" % jb) for jb in range(JB)]
         for g in range(PASSES):
             for jb in range(JB):
-                mm(yo[jb][:], 0, g, jb)
-        cast(nc.scalar.copy, (1, 0), 0, N, "bf_c")
-        quant((1, 0))
-        cast(nc.vector.tensor_copy, (1, 1), 0, V_SHARE, "bf_b")
-        cast(nc.scalar.copy, (1, 1), V_SHARE, N, "bf_b")
-        quant((1, 1))
+                mm(yo[jb][:], W1, g, jb)
+        new_bf((W2, 0), "bf_c")
+        cast(nc.scalar.copy, (W2, 0), 0, N)
+        quant((W2, 0))
+        c_sq = sb.tile([P, JB], F32, name="c_sq", tag="stage_m0")
+        c_4 = sb.tile([P, JB], F32, name="c_4")
+        nc.scalar.activation(c_sq[:], lf_col[:], ACT.Square, scale=-0.5, bias=1.0)
+        nc.scalar.activation(c_4[:], c_sq[:], ACT.Square)
+        new_bf((W2, 1), "bf_b")
+        cast(nc.vector.tensor_copy, (W2, 1), 0, V_SHARE)
+        cast(nc.scalar.copy, (W2, 1), V_SHARE, N)
+        quant((W2, 1))
+        inv_c_sq = sb.tile([P, JB], F32, name="inv_c_sq", tag="stage_m1")
+        nc.scalar.activation(inv_c_sq[:], c_4[:], ACT.Abs_reciprocal_sqrt)
         for jb in range(JB):
             for g in range(PASSES):
-                mm(yi[jb][:], 1, g, jb)
+                mm(yi[jb][:], W2, g, jb)
 
-        csq = sb.tile([P, JB], F32, name="csq", tag="w_raw11")
-        a_neg = sb.tile([P, JB], F32, name="a_neg")
-        nc.scalar.activation(csq[:], lf_col[:], ACT.Square, scale=-0.5, bias=1.0)
-        nz = sb.tile([P, JB, N], F32, name="nz", tag="bf_b", align_bytes=64)
+        z_s = sb.tile([P, JB, N], F32, name="z_s", tag="bf_b", align_bytes=64)
         lp = sb.tile([P, JB, N], F32, name="lp")
         sq = sb.tile([P, JB, N], F32, name="sq", tag="sq")
         rs = sb.tile([P, JB, N], F32, name="rs")
 
-        def make_nz(jb):
-            nc.vector.scalar_tensor_tensor(nz[:, jb, :], yo[jb][:], -0.8, g_t[:, jb, :], ALU.mult, ALU.subtract)
+        def make_z(jb):
+            nc.vector.scalar_tensor_tensor(z_s[:, jb, :], yo[jb][:], 0.8, log_t[:, jb, :], ALU.mult, ALU.add)
 
-        make_nz(0)
+        make_z(0)
         for jb in range(JB):
-            if jb + 1 < JB:
-                make_nz(jb + 1)
-            nc.vector.scalar_tensor_tensor(lp[:, jb, :], yi[jb][:], -0.8, nz[:, jb, :], ALU.mult, ALU.subtract)
-            if jb + 1 < JB:
-                nc.scalar.activation(sq[:, jb, :], lp[:, jb, :], ACT.Square)
-            else:
+            last = jb == JB - 1
+            if not last:
+                make_z(jb + 1)
+            nc.vector.scalar_tensor_tensor(lp[:, jb, :], yi[jb][:], -0.8, z_s[:, jb, :], ALU.mult, ALU.add)
+            if last:
                 nc.vector.tensor_tensor(sq[:, jb, :], lp[:, jb, :], lp[:, jb, :], ALU.mult)
-            nc.scalar.activation(rs[:, jb, :], sq[:, jb, :], ACT.Abs_reciprocal_sqrt, bias=csq[:, jb : jb + 1])
+            else:
+                nc.scalar.activation(sq[:, jb, :], lp[:, jb, :], ACT.Square)
+            nc.scalar.activation(
+                rs[:, jb, :], sq[:, jb, :], ACT.Abs_reciprocal_sqrt, scale=inv_c_sq[:, jb : jb + 1], bias=1.0
+            )
 
-        arg = sb.tile([P, JB, N], F32, name="arg")
-        nc.vector.tensor_scalar(arg[:], lp[:], -(CLAMP + SHIFT), None, ALU.max)
-        arg_t = [ps.tile([P, JB, P], F32, name="arg_t%d" % m, tag="a%d" % m) for m in range(MB)]
+        neg_x = sb.tile([P, JB, N], F32, name="neg_x")
+        nc.vector.tensor_scalar(neg_x[:], lp[:], -1.0, CLAMP + SHIFT, ALU.mult, ALU.min)
+        neg_x_bank = [ps.tile([P, JB, P], F32, name="neg_x_bank%d" % m, tag="a%d" % m) for m in range(MB)]
         for m in range(MB):
             for jb in range(JB):
-                nc.tensor.transpose(arg_t[m][:, jb, :], arg[:, jb, m * P : (m + 1) * P], ident[:])
+                nc.tensor.transpose(neg_x_bank[m][:, jb, :], neg_x[:, jb, m * P : (m + 1) * P], ident[:])
         ex = sb.tile([P, MB, S], F32, name="ex", tag="sq")
         for m in range(MB):
-            nc.scalar.activation(
-                ex[:, m, :], arg_t[m][:].rearrange("p b j -> p (b j)"), ACT.Exp, scale=-1.0, bias=-SHIFT
-            )
+            nc.scalar.activation(ex[:, m, :], neg_x_bank[m][:].rearrange("p b j -> p (b j)"), ACT.Exp, bias=-SHIFT)
 
-        nc.vector.scalar_tensor_tensor(a_neg[:], csq[:], -1.0, lf_col[:], ALU.mult, ALU.mult)
-        nlf = sb.tile([P, JB, N], F32, name="nlf")
+        lf = sb.tile([P, JB, N], F32, name="lf")
         for jb in range(JB):
             nc.vector.scalar_tensor_tensor(
-                nlf[:, jb, :], rs[:, jb, :], a_neg[:, jb : jb + 1], rs[:, jb, :], ALU.mult, ALU.mult
+                lf[:, jb, :], rs[:, jb, :], lf_col[:, jb : jb + 1], rs[:, jb, :], ALU.mult, ALU.mult
             )
-        pieces = [(m, h) for m in range(MB) for h in range(2)]
-        acc = [ps.tile([P, JB, P], F32, name="acc%d" % m, tag="b%d" % (2 + m)) for m in range(MB)]
-        for term, src in enumerate((nz, arg, nlf)):
+
+        acc = [ps.tile([P, JB, P], F32, name="acc%d" % m, tag="b%d" % (JB - MB + m)) for m in range(MB)]
+        terms = (z_s, neg_x, lf)
+        for n, term in enumerate(terms):
             for m in range(MB):
                 for jb in range(JB):
                     nc.tensor.matmul(
                         acc[m][:, jb, :],
-                        src[:, jb, m * P : (m + 1) * P],
+                        term[:, jb, m * P : (m + 1) * P],
                         ident[:],
                         is_transpose=True,
-                        start=term == 0 and jb == 0,
-                        stop=term == 2 and jb == JB - 1,
+                        start=n == 0 and jb == 0,
+                        stop=n == len(terms) - 1 and jb == JB - 1,
                     )
-        for m, h in pieces:
-            cols = slice(2 * h * P, 2 * (h + 1) * P)
-            soft = sb.tile([P, 2 * P], F32, name="soft%d%d" % (m, h))
-            nc.scalar.activation(soft[:], ex[:, m, cols], ACT.Ln, bias=1.0)
-            res = sb.tile([P, 2 * P], F32, name="res%d%d" % (m, h))
-            nc.vector.scalar_tensor_tensor(
-                res[:], acc[m][:].rearrange("p b j -> p (b j)")[:, cols], -1.0, soft[:], ALU.mult, ALU.subtract
-            )
-            nc.sync.dma_start(out=out[m * P : (m + 1) * P, cols], in_=res[:])
+
+        for m in range(MB):
+            for h in range(2):
+                cols = slice(h * S // 2, (h + 1) * S // 2)
+                soft = sb.tile([P, S // 2], F32, name="soft%d%d" % (m, h))
+                nc.scalar.activation(soft[:], ex[:, m, cols], ACT.Ln, bias=1.0)
+                res = sb.tile([P, S // 2], F32, name="res%d%d" % (m, h))
+                nc.vector.tensor_tensor(
+                    res[:], acc[m][:].rearrange("p b j -> p (b j)")[:, cols], soft[:], ALU.subtract
+                )
+                nc.sync.dma_start(out=out[m * P : (m + 1) * P, cols], in_=res[:])

import math
from contextlib import ExitStack

import concourse.mybir as mybir

K, T, S, N, R = 1024, 1024, 512, 256, 256
FLOPS = 2 * 2 * K * S * N

F32 = mybir.dt.float32
BF16 = mybir.dt.bfloat16
I32 = mybir.dt.int32
U32 = mybir.dt.uint32
U16 = mybir.dt.uint16
U8 = mybir.dt.uint8
FP8X4 = mybir.dt.float8_e4m3fn_x4
ALU = mybir.AluOpType
ACT = mybir.ActivationFunctionType

P = 128
QUAD = 32
PACK = 4
K_PASS = P * PACK
PASSES = K // K_PASS
JB = S // P
MB = N // P
LINE = 4
SHIFT = 0.4
CLAMP = 40.0
WINDOW = 704
V_SHARE = 160
W1, W2 = 0, 1


def tile_picked_ytroef_log_p_kernel(
    tc, x_words, x_scales, w1, w2, mcon, lfc, offs, bath, out
):
    nc = tc.nc
    with ExitStack() as ctx:
        sb = ctx.enter_context(tc.tile_pool(name="sb", bufs=1))
        ps = ctx.enter_context(tc.psum_pool(name="ps", bufs=1))

        s_tab = sb.tile([P, T], U8, name="s_tab", tag="scales", align_bytes=64)
        nc.vector.memset(s_tab[:].bitcast(I32), 0)

        ident = sb.tile([P, P], F32, name="ident")
        ones = sb.tile([P, P], F32, name="ones", tag="stage_a")
        col = sb.tile([P, P], F32, name="col", tag="stage_b", align_bytes=64)
        lane = sb.tile([P, QUAD], F32, name="lane", align_bytes=64)
        quad_base = sb.tile([P, 1], F32, name="quad_base")
        nc.vector.memset(ones[:], 1.0)
        for q in range(P // QUAD):
            nc.vector.memset(quad_base[QUAD * q : QUAD * (q + 1), :], float(QUAD * q))
        nc.vector.tensor_tensor_scan(col[:], ones[:], ones[:], -1.0, ALU.mult, ALU.add)
        nc.vector.transpose(lane[:], col[:, 0:QUAD])
        nc.vector.tensor_scalar(ident[:], col[:], quad_base[:, 0:1], lane[:, 0:1], ALU.subtract, ALU.is_equal)

        offs_t = sb.tile([P, S // 16], U16, name="offs_t")
        bath_t = sb.tile([P, S // 16], U16, name="bath_t")
        m_tab = [sb.tile([P, R], F32, name="m_tab%d" % m, tag="stage_m%d" % m) for m in range(MB)]
        lf_col = sb.tile([P, JB], F32, name="lf_col")
        x_tab = {}
        w_raw = {}

        def load_w(a, g, tag):
            w_raw[a, g] = sb.tile([P, PACK, N], F32, name="w_raw%d%d" % (a, g), tag=tag)
            rows = (w1, w2)[a][g * K_PASS : (g + 1) * K_PASS, :]
            nc.sync.dma_start(out=w_raw[a, g][:], in_=rows.rearrange("(p t) n -> p t n", t=PACK))

        def load_x(g, tag):
            x_tab[g] = sb.tile([P, T], I32, name="x_tab%d" % g, tag=tag, align_bytes=64)
            nc.sync.dma_start(out=x_tab[g][:], in_=x_words[g].rearrange("p n t -> p (n t)").bitcast(I32))

        nc.sync.dma_start(out=m_tab[0][:], in_=mcon[0:P, :])
        nc.sync.dma_start(bath_t[:], bath)
        nc.sync.dma_start(out=m_tab[1][:], in_=mcon[P : 2 * P, :])
        load_w(W1, 0, "w_first")
        nc.sync.dma_start(offs_t[:], offs)
        load_x(0, "x_first")
        for q in range(P // QUAD):
            nc.sync.dma_start(
                out=s_tab[QUAD * q : QUAD * q + 4 * PASSES, :].bitcast(I32),
                in_=x_scales[:, 4 * q : 4 * q + 4, :].bitcast(I32),
            )
        load_w(W1, 1, "stage_a")
        load_x(1, "stage_b")
        with nc.allow_non_contiguous_dma(reason="one factor to a partition"):
            nc.gpsimd.dma_start(out=lf_col[:], in_=lfc[0:1, :].rearrange("o (b p) -> p (o b)", p=P))

        m_log = sb.tile([P, R + WINDOW], F32, name="m_log")
        nc.vector.memset(m_log[:, MB * R :], 0.0)
        m_at = [(MB - 1 - m) * R for m in range(MB)]
        for m in range(MB):
            nc.scalar.activation(m_log[:, m_at[m] : m_at[m] + R], m_tab[m][:], ACT.Ln, scale=math.exp(-SHIFT))
        load_w(W2, 0, "stage_m0")
        load_w(W2, 1, "stage_m1")

        log_mb = [sb.tile([P, S], F32, name="log_mb%d" % m) for m in range(MB)]
        for m in range(MB):
            nc.vector.tensor_copy(log_mb[m][:], m_log[:, m_at[m] : m_at[m] + WINDOW].indirect(bath_t[:]))
        log_bank = [ps.tile([P, 2, N], F32, name="log_bank%d" % h, tag="b%d" % h) for h in range(JB // 2)]
        for m in range(MB):
            for jb in range(JB):
                nc.tensor.transpose(
                    log_bank[jb // 2][:, jb % 2, m * P : (m + 1) * P],
                    log_mb[m][:, jb * P : (jb + 1) * P],
                    ident[:],
                )

        x_cd = {}
        x_sc = sb.tile([P, S], U8, name="x_sc", align_bytes=64)
        w_bf = {}
        w_cd = {key: sb.tile([P, N], U32, name="w_cd%d%d" % key, align_bytes=64) for key in sorted(w_raw)}

        def new_bf(key, tag):
            w_bf[key] = sb.tile([P, N, PACK], BF16, name="w_bf%d%d" % key, tag=tag, align_bytes=64)

        def cast(copy, key, lo, hi):
            copy(
                w_bf[key][:, lo:hi, :].rearrange("p (c i) t -> p c t i", i=LINE),
                w_raw[key][:, :, lo:hi].rearrange("p t (c i) -> p c t i", i=LINE),
            )

        def gather_x(g, tag):
            x_cd[g] = sb.tile([P, S], U32, name="x_cd%d" % g, tag=tag, align_bytes=64)
            nc.vector.tensor_copy(x_cd[g][:], x_tab[g][:].bitcast(U32).indirect(offs_t[:]))

        new_bf((W1, 0), "bf_a")
        cast(nc.scalar.copy, (W1, 0), 0, N)
        gather_x(0, "x_codes")
        nc.vector.tensor_copy(x_sc[:], s_tab[:].indirect(offs_t[:]))

        w_scales = sb.tile([P, 2 * PASSES * N], U8, name="w_scales", tag="scales", align_bytes=64)
        w_sc = {key: w_scales[:, n * N : (n + 1) * N] for n, key in enumerate(sorted(w_raw))}

        def quant(key):
            nc.vector.quantize_mx(
                out=w_cd[key][:].bitcast(FP8X4), scales=w_sc[key], in_=w_bf[key][:].rearrange("p n t -> p (n t)")
            )

        def mm(dst, a, g, jb):
            cols = slice(jb * P, (jb + 1) * P)
            nc.tensor.matmul_mx(
                out=dst,
                lhsT=x_cd[g][:, cols].bitcast(FP8X4),
                lhsT_scale=x_sc[4 * g :, cols],
                rhs=w_cd[a, g][:].bitcast(FP8X4),
                rhs_scale=w_sc[a, g],
                start=(g == 0),
                stop=(g == PASSES - 1),
            )

        quant((W1, 0))
        new_bf((W1, 1), "bf_b")
        cast(nc.scalar.copy, (W1, 1), 0, N)
        log_t = sb.tile([P, JB, N], F32, name="log_t", tag="stage_a")
        for h in range(JB // 2):
            nc.scalar.copy(log_t[:, 2 * h : 2 * h + 2, :], log_bank[h][:])
        gather_x(1, "bf_a")
        quant((W1, 1))
        yo = [ps.tile([P, N], F32, name="yo%d" % jb, tag="a%d" % jb) for jb in range(JB)]
        yi = [ps.tile([P, N], F32, name="yi%d" % jb, tag="b%d" % jb) for jb in range(JB)]
        for g in range(PASSES):
            for jb in range(JB):
                mm(yo[jb][:], W1, g, jb)
        new_bf((W2, 0), "bf_c")
        cast(nc.scalar.copy, (W2, 0), 0, N)
        quant((W2, 0))
        c_sq = sb.tile([P, JB], F32, name="c_sq", tag="stage_m0")
        c_4 = sb.tile([P, JB], F32, name="c_4")
        nc.scalar.activation(c_sq[:], lf_col[:], ACT.Square, scale=-0.5, bias=1.0)
        nc.scalar.activation(c_4[:], c_sq[:], ACT.Square)
        new_bf((W2, 1), "bf_b")
        cast(nc.vector.tensor_copy, (W2, 1), 0, V_SHARE)
        cast(nc.scalar.copy, (W2, 1), V_SHARE, N)
        quant((W2, 1))
        inv_c_sq = sb.tile([P, JB], F32, name="inv_c_sq", tag="stage_m1")
        nc.scalar.activation(inv_c_sq[:], c_4[:], ACT.Abs_reciprocal_sqrt)
        for jb in range(JB):
            for g in range(PASSES):
                mm(yi[jb][:], W2, g, jb)

        z_s = sb.tile([P, JB, N], F32, name="z_s", tag="bf_b", align_bytes=64)
        lp = sb.tile([P, JB, N], F32, name="lp")
        sq = sb.tile([P, JB, N], F32, name="sq", tag="sq")
        rs = sb.tile([P, JB, N], F32, name="rs")

        def make_z(jb):
            nc.vector.scalar_tensor_tensor(z_s[:, jb, :], yo[jb][:], 0.8, log_t[:, jb, :], ALU.mult, ALU.add)

        make_z(0)
        for jb in range(JB):
            last = jb == JB - 1
            if not last:
                make_z(jb + 1)
            nc.vector.scalar_tensor_tensor(lp[:, jb, :], yi[jb][:], -0.8, z_s[:, jb, :], ALU.mult, ALU.add)
            if last:
                nc.vector.tensor_tensor(sq[:, jb, :], lp[:, jb, :], lp[:, jb, :], ALU.mult)
            else:
                nc.scalar.activation(sq[:, jb, :], lp[:, jb, :], ACT.Square)
            nc.scalar.activation(
                rs[:, jb, :], sq[:, jb, :], ACT.Abs_reciprocal_sqrt, scale=inv_c_sq[:, jb : jb + 1], bias=1.0
            )

        neg_x = sb.tile([P, JB, N], F32, name="neg_x")
        nc.vector.tensor_scalar(neg_x[:], lp[:], -1.0, CLAMP + SHIFT, ALU.mult, ALU.min)
        neg_x_bank = [ps.tile([P, JB, P], F32, name="neg_x_bank%d" % m, tag="a%d" % m) for m in range(MB)]
        for m in range(MB):
            for jb in range(JB):
                nc.tensor.transpose(neg_x_bank[m][:, jb, :], neg_x[:, jb, m * P : (m + 1) * P], ident[:])
        ex = sb.tile([P, MB, S], F32, name="ex", tag="sq")
        for m in range(MB):
            nc.scalar.activation(ex[:, m, :], neg_x_bank[m][:].rearrange("p b j -> p (b j)"), ACT.Exp, bias=-SHIFT)

        lf = sb.tile([P, JB, N], F32, name="lf")
        for jb in range(JB):
            nc.vector.scalar_tensor_tensor(
                lf[:, jb, :], rs[:, jb, :], lf_col[:, jb : jb + 1], rs[:, jb, :], ALU.mult, ALU.mult
            )

        acc = [ps.tile([P, JB, P], F32, name="acc%d" % m, tag="b%d" % (JB - MB + m)) for m in range(MB)]
        terms = (z_s, neg_x, lf)
        for n, term in enumerate(terms):
            for m in range(MB):
                for jb in range(JB):
                    nc.tensor.matmul(
                        acc[m][:, jb, :],
                        term[:, jb, m * P : (m + 1) * P],
                        ident[:],
                        is_transpose=True,
                        start=n == 0 and jb == 0,
                        stop=n == len(terms) - 1 and jb == JB - 1,
                    )

        for m in range(MB):
            for h in range(2):
                cols = slice(h * S // 2, (h + 1) * S // 2)
                soft = sb.tile([P, S // 2], F32, name="soft%d%d" % (m, h))
                nc.scalar.activation(soft[:], ex[:, m, cols], ACT.Ln, bias=1.0)
                res = sb.tile([P, S // 2], F32, name="res%d%d" % (m, h))
                nc.vector.tensor_tensor(
                    res[:], acc[m][:].rearrange("p b j -> p (b j)")[:, cols], soft[:], ALU.subtract
                )
                nc.sync.dma_start(out=out[m * P : (m + 1) * P, cols], in_=res[:])
